import numpy as np
import ml_dtypes


def mxq(x, axis, fmt="e4m3"):
    dtype, down = {"e4m3": (ml_dtypes.float8_e4m3fn, 7), "e5m2": (ml_dtypes.float8_e5m2, 14)}[fmt]
    v = np.moveaxis(np.asarray(x, np.float32).astype(ml_dtypes.bfloat16).astype(np.float64), axis, -1)
    blocks = v.reshape(v.shape[:-1] + (-1, 32))
    amax = np.abs(blocks).max(-1, keepdims=True)
    byte = np.maximum(np.where(amax > 0, np.frexp(amax)[1] - 1 + 127, 0) - down, 1)
    scale = np.exp2(byte - 127.0)
    codes = (blocks / scale).astype(np.float32).astype(dtype).astype(np.float64)
    return np.moveaxis((codes * scale).reshape(v.shape), -1, axis)


WIDE = False


def mx_kscale(k):
    if not WIDE:
        return np.ones(k)
    levels = np.array([30, -30])
    if k % 512:
        return np.exp2(np.random.permutation(np.resize(levels, k // 32))).repeat(32)
    a = np.empty((k // 512, 16))
    for p in range(k // 512):
        a[p, :8] = np.random.permutation(np.resize(levels, 8))
        for g in range(8):
            far = levels[np.abs(levels - a[p, g]) >= 10]
            a[p, g + 8] = far[np.random.randint(len(far))]
    return np.exp2(a.ravel()).repeat(32)


def f64(x):
    return np.asarray(x).astype(np.float64)


def striped(idx):
    return np.tile(np.asarray(idx).reshape(-1, 16).T, (8, 1)).astype(np.uint16)


def unstriped(offs):
    return offs[:16].T.reshape(-1).astype(np.int64)


E2M1 = np.array([0.0, 0.5, 1.0, 1.5, 2.0, 3.0, 4.0, 6.0, -0.0, -0.5, -1.0, -1.5, -2.0, -3.0, -4.0, -6.0])


def pack_weight(w, fmt):
    k, n = w.shape
    w = f64(np.asarray(w, np.float32).astype(ml_dtypes.bfloat16)).reshape(k // 32, 32, n)
    amax = np.abs(w).max(1)
    if fmt == "e4m3":
        byte = np.frexp(amax)[1] - 1 + 127 - 7
    else:
        mant, ex = np.frexp(amax / 6.0)
        byte = np.where(mant > 0.5, ex, ex - 1) + 127
    byte = np.clip(np.where(amax > 0, byte, 1), 1, 254)
    scaled = (w * np.exp2(127.0 - byte)[:, None, :]).reshape(k, n).astype(np.float32)
    by_word = np.ascontiguousarray(scaled.reshape(k // 512, 128, 4, n).transpose(0, 1, 3, 2))
    if fmt == "e4m3":
        words = by_word.astype(ml_dtypes.float8_e4m3fn).view(np.uint8)
    else:
        c = by_word.astype(ml_dtypes.float4_e2m1fn).view(np.uint8) & 0xF
        words = (c[..., 0::2] | (c[..., 1::2] << 4)).reshape(k // 512, 128, 2 * n)
    return np.ascontiguousarray(words), np.ascontiguousarray(byte.astype(np.uint8).reshape(k // 512, 16, n))


def unpack_weight(words, scales, fmt):
    g, _, n = scales.shape
    words = np.ascontiguousarray(words).reshape(g, 128, n, -1)
    if fmt == "e4m3":
        vals = words.view(ml_dtypes.float8_e4m3fn).astype(np.float64)
    else:
        nib = np.empty((g, 128, n, 4), np.uint8)
        nib[..., 0::2] = words & 0xF
        nib[..., 1::2] = words >> 4
        vals = E2M1[nib]
    vals = vals * np.repeat(np.exp2(scales.astype(np.float64) - 127.0), 8, axis=1)[..., None]
    return vals.transpose(0, 1, 3, 2).reshape(g * 512, n)


def bf(x):
    return np.asarray(x, np.float32).astype(ml_dtypes.bfloat16)


def planes(Y):
    r, m = Y.shape
    b = f64(bf(Y)).reshape(r // 32, 32, m)
    amax = np.abs(b).max(1)
    byte = np.clip(np.where(amax > 0, np.frexp(amax)[1] - 1 + 127 - 7, 1), 1, 254)
    codes = (b * np.exp2(127.0 - byte)[:, None, :]).reshape(r, m).astype(np.float32).astype(ml_dtypes.float8_e4m3fn).view(np.uint8)
    words = codes.reshape(r // 512, 128, 4, m).transpose(0, 1, 3, 2)
    return np.ascontiguousarray(words), np.ascontiguousarray(byte.astype(np.uint8).reshape(r // 512, 16, m))


K, T, J, B, R, V, N, Z = 1024, 1024, 256, 32, 512, 512, 512, 512


def setup_inputs():
    n = np.random.standard_normal
    idx = np.random.permutation(T)[:J]
    idx2 = np.random.permutation(V)[:J]
    idx3 = np.random.permutation(V)[:J]
    idx4 = np.random.permutation(Z)[:J]
    fk = mx_kscale(K)
    fr = mx_kscale(R)
    wp = pack_weight(n((K, R)) * 1 / np.sqrt(K) * fk[:, None] * fr, "e4m3")
    wbp = pack_weight(n((R, N)) * 1 / np.sqrt(R) / fr[:, None], "e2m1")
    return {
        "xf": (n((K, T))).astype(np.float32),
        "fk": (np.random.uniform(0.5, 2.0, (K, 1)) / fk[:, None]).astype(np.float32),
        "w_words": wp[0],
        "w_scales": wp[1],
        "tb": (n((R, V)) * 0.7 * fr[:, None]).astype(np.float32),
        "wb_words": wbp[0],
        "wb_scales": wbp[1],
        "tz": (n((N, Z)) * 0.6).astype(np.float32),
        "rw": (np.random.uniform(0.5, 2.0, (1, J))).astype(np.float32),
        "offs": striped(idx),
        "offs2": striped(idx2),
        "offs3": striped(idx3),
        "offs4": striped(idx4),
    }


def reference(xf, fk, w_words, w_scales, tb, wb_words, wb_scales, tz, rw, offs, offs2, offs3, offs4):
    idx = unstriped(offs)
    idx2 = unstriped(offs2)
    idx3 = unstriped(offs3)
    idx4 = unstriped(offs4)
    wu = unpack_weight(w_words, w_scales, "e4m3")
    wbu = unpack_weight(wb_words, wb_scales, "e2m1")
    xg = f64(xf)[:, idx]
    g1 = xg.reshape(K, B, J // B).mean(axis=2)
    g2 = np.repeat(g1, J // B, axis=1)
    u = (xg - g2) * f64(fk)
    uq = mxq(u, 0, "e4m3")
    a = wu.T @ uq
    hid = np.maximum(a + f64(tb)[:, idx2] - f64(tb)[:, idx3], 0.0)
    hidq = mxq(hid, 0, "e5m2")
    p = wbu.T @ hidq
    y = np.maximum(p, f64(tz)[:, idx4]) * f64(rw)
    words, scales = planes(y)
    return y, words, scales

@@ -1,0 +1,287 @@
+from contextlib import ExitStack
+
+import concourse.mybir as mybir
+from concourse.masks import make_identity
+
+K, T, J, R, V, N, Z = 1024, 1024, 256, 512, 512, 512, 512
+GROUP = 8
+FLOPS = 2 * K * R * J + 2 * R * N * J
+
+F32 = mybir.dt.float32
+BF16 = mybir.dt.bfloat16
+I32 = mybir.dt.int32
+U16 = mybir.dt.uint16
+U8 = mybir.dt.uint8
+E4M3 = mybir.dt.float8_e4m3fn_x4
+E5M2 = mybir.dt.float8_e5m2_x4
+E2M1 = mybir.dt.float4_e2m1fn_x4
+ALU = mybir.AluOpType
+COPY = mybir.ActivationFunctionType.Copy
+AXIS_X = mybir.AxisListType.X
+
+P = 128
+PACK = 4
+PASSES = K // (P * PACK)
+HALF = J // 2
+HALVES = 2
+
+
+def tile_list_centredpicks_tworeach_floored_pl_kernel(
+    tc, xf, fk, w_words, w_scales, tb, wb_words, wb_scales, tz, rw, offs, offs2, offs3, offs4, out_0, out_1, out_2
+):
+    nc = tc.nc
+    with ExitStack() as ctx:
+        pool = ctx.enter_context(tc.tile_pool(name="held", bufs=1))
+        psum = ctx.enter_context(tc.psum_pool(name="psum", bufs=1))
+
+        def sbuf(name, shape, dtype):
+            return pool.tile(shape, dtype, name=name, align_bytes=64)
+
+        def cols(h):
+            return slice(h * HALF, (h + 1) * HALF)
+
+        list_x = sbuf("list_x", [P, J // 16], U16)
+        list_plus = sbuf("list_plus", [P, J // 16], U16)
+        list_minus = sbuf("list_minus", [P, J // 16], U16)
+        list_floor = sbuf("list_floor", [P, J // 16], U16)
+
+        x_rows = xf.rearrange("(g p t) c -> g t p c", g=PASSES, t=PACK)
+        tb_rows = tb.rearrange("(p t) c -> t p c", t=PACK)
+        tz_rows = tz.rearrange("(p t) c -> t p c", t=PACK)
+        x_win = [[sbuf("x_win%d%d" % (g, t), [P, T], F32) for t in range(PACK)] for g in range(PASSES)]
+        tb_win = [sbuf("tb_win%d" % t, [P, V], F32) for t in range(PACK)]
+        tz_win = [sbuf("tz_win%d" % t, [P, Z], F32) for t in range(PACK)]
+        w_raw = sbuf("w_raw", [P, PASSES, R], I32)
+        wb_raw = sbuf("wb_raw", [P, 2 * N], U8)
+        scale_raw = sbuf("scale_raw", [P, PASSES, R], U8)
+        scale_b_raw = sbuf("scale_b_raw", [P, N], U8)
+        fk_sb = sbuf("fk_sb", [P, PASSES, PACK], F32)
+        rw_col = sbuf("rw_col", [P, HALVES], F32)
+
+        nc.vector.memset(scale_raw[:].rearrange("p s c -> p (s c)").bitcast(I32), 0)
+        nc.vector.memset(scale_b_raw[:].bitcast(I32), 0)
+
+        def load_x(g, t):
+            nc.sync.dma_start(out=x_win[g][t][:], in_=x_rows[g, t])
+
+        def load_w_scales(q):
+            nc.sync.dma_start(
+                out=scale_raw[32 * q : 32 * q + 4].bitcast(I32),
+                in_=w_scales[:, 4 * q : 4 * q + 4, :].rearrange("g r c -> r g c").bitcast(I32),
+            )
+
+        def load_wb_scales(q):
+            nc.sync.dma_start(
+                out=scale_b_raw[32 * q : 32 * q + 4, :].bitcast(I32),
+                in_=wb_scales[0, 4 * q : 4 * q + 4, :].bitcast(I32),
+            )
+
+        nc.sync.dma_start(list_x[:], offs)
+        load_x(0, 0)
+        nc.sync.dma_start(out=fk_sb[:], in_=fk.rearrange("(g p t) o -> p g (t o)", g=PASSES, t=PACK))
+        nc.sync.dma_start(out=w_raw[:], in_=w_words.rearrange("g p c t -> p g (c t)").bitcast(I32))
+        load_x(0, 1)
+        nc.sync.dma_start(out=wb_raw[:].bitcast(I32), in_=wb_words[0].bitcast(I32))
+        load_w_scales(0)
+        load_x(0, 2)
+        load_w_scales(1)
+        load_w_scales(2)
+        load_x(0, 3)
+        load_w_scales(3)
+        nc.sync.dma_start(list_minus[:], offs3)
+        nc.sync.dma_start(out=tb_win[0][:], in_=tb_rows[0])
+        nc.sync.dma_start(list_plus[:], offs2)
+        load_x(1, 0)
+        load_wb_scales(0)
+        nc.sync.dma_start(out=tb_win[1][:], in_=tb_rows[1])
+        load_wb_scales(1)
+        load_x(1, 1)
+        load_wb_scales(2)
+        nc.sync.dma_start(out=tb_win[2][:], in_=tb_rows[2])
+        load_wb_scales(3)
+        load_x(1, 2)
+        load_x(1, 3)
+        nc.sync.dma_start(out=tb_win[3][:], in_=tb_rows[3])
+        nc.sync.dma_start(list_floor[:], offs4)
+        with nc.allow_non_contiguous_dma(reason="one weight a partition"):
+            nc.sync.dma_start(out=rw_col[:], in_=rw.rearrange("o (h p) -> p (o h)", h=HALVES))
+        for t in range(PACK):
+            nc.sync.dma_start(out=tz_win[t][:], in_=tz_rows[t])
+
+        ident = sbuf("ident", [P, P], F32)
+        make_identity(nc, ident[:])
+        rw_all = psum.tile([P, J], F32, name="rw_all")
+        for h in range(HALVES):
+            nc.tensor.transpose(rw_all[:, cols(h)], rw_col[:, h : h + 1].to_broadcast([P, P]), ident[:])
+
+        w_dealt = sbuf("w_dealt", [P, PASSES, PACK, P], I32)
+        wb_dealt = sbuf("wb_dealt", [P, PACK, 2 * P], U8)
+        scale_dealt = sbuf("scale_dealt", [P, PASSES, PACK, P], U8)
+        scale_b_dealt = sbuf("scale_b_dealt", [P, PACK, P], U8)
+        for g in range(PASSES):
+            nc.vector.tensor_copy(
+                out=w_dealt[:, g].rearrange("p t (c i) -> p c t i", i=4),
+                in_=w_raw[:, g].rearrange("p (c i t) -> p c t i", i=4, t=PACK),
+            )
+        nc.vector.tensor_copy(
+            out=wb_dealt[:].rearrange("p t (c i b) -> p c t i b", i=8, b=2),
+            in_=wb_raw[:].rearrange("p (c i t b) -> p c t i b", i=8, t=PACK, b=2),
+        )
+
+        picked = [sbuf("picked%d" % g, [P, PACK, J], F32) for g in range(PASSES)]
+        sums = [sbuf("sums%d" % g, [P, PACK, J // GROUP], F32) for g in range(PASSES)]
+        scaled = sbuf("scaled", [P, PACK, J], F32)
+        means = sbuf("means", [P, PACK, J // GROUP], F32)
+        centred = sbuf("centred", [P, PACK, J], F32)
+        u0_bf = sbuf("u0_bf", [P, J, PACK], BF16)
+        u0_codes = sbuf("u0_codes", [P, J], I32)
+        u0_scales = sbuf("u0_scales", [P, J], U8)
+        u1_bf = [sbuf("u1_bf%d" % h, [P, HALF, PACK], BF16) for h in range(HALVES)]
+        u1_codes = [sbuf("u1_codes%d" % h, [P, HALF], I32) for h in range(HALVES)]
+        u1_scales = [sbuf("u1_scales%d" % h, [P, HALF], U8) for h in range(HALVES)]
+        u_codes = [[u0_codes[:, cols(h)] for h in range(HALVES)], [u1_codes[h][:] for h in range(HALVES)]]
+        u_scales = [[u0_scales[:, cols(h)] for h in range(HALVES)], [u1_scales[h][:] for h in range(HALVES)]]
+        minus = sbuf("minus", [P, PACK, J], F32)
+        reach = sbuf("reach", [P, PACK, J], F32)
+        floor = sbuf("floor", [P, PACK, J], F32)
+
+        def pick(g, t):
+            nc.scalar.activation(picked[g][:, t, :], x_win[g][t][:].indirect(list_x[:]), COPY)
+
+        def grouped(ap):
+            return ap.rearrange("p t (b i) -> p (t b) i", i=GROUP)
+
+        def group_sums(g, source, planes):
+            nc.vector.tensor_reduce(
+                sums[g][:, planes, :].rearrange("p t b -> p (t b)"), grouped(source[:, planes, :]), AXIS_X, ALU.add
+            )
+
+        def centre(planes):
+            group_sums(1, picked[1], planes)
+            count = (planes.stop - planes.start) * J // GROUP
+            nc.vector.scalar_tensor_tensor(
+                out=grouped(centred[:, planes, :]),
+                in0=sums[1][:, planes, :].rearrange("p t b -> p (t b)").unsqueeze(2).to_broadcast([P, count, GROUP]),
+                scalar=-1.0 / GROUP,
+                in1=grouped(picked[1][:, planes, :]),
+                op0=ALU.mult,
+                op1=ALU.add,
+            )
+
+        def woven(tile):
+            return tile[:].rearrange("p (c i) t -> p c t i", i=4)
+
+        def planar(ap):
+            return ap.rearrange("p t (c i) -> p c t i", i=4)
+
+        def quantise(codes, scales, values, fmt):
+            nc.vector.quantize_mx(out=codes.bitcast(fmt), scales=scales, in_=values[:].rearrange("p j t -> p (j t)"))
+
+        def reach_plane(t):
+            nc.scalar.activation(minus[:, t, :], tb_win[t][:].indirect(list_minus[:]), COPY)
+            nc.vector.tensor_tensor(reach[:, t, :], tb_win[t][:].indirect(list_plus[:]), minus[:, t, :], ALU.subtract)
+
+        a_bank = [psum.tile([P, PACK, HALF], F32, name="a_bank%d" % h) for h in range(HALVES)]
+
+        def first_product(g, h):
+            for t in range(PACK):
+                nc.tensor.matmul_mx(
+                    out=a_bank[h][:, t, :],
+                    lhsT=w_dealt[:, g, t, :].bitcast(E4M3),
+                    lhsT_scale=scale_dealt[:, g, t, :],
+                    rhs=u_codes[g][h].bitcast(E4M3),
+                    rhs_scale=u_scales[g][h],
+                    start=(g == 0 and t == 0),
+                    stop=(g == PASSES - 1 and t == PACK - 1),
+                )
+
+        for t in range(PACK):
+            pick(0, t)
+            nc.scalar.activation(scaled[:, t, :], picked[0][:, t, :], COPY, scale=fk_sb[:, 0, t : t + 1])
+            if t % 2:
+                group_sums(0, scaled, slice(t - 1, t + 1))
+        nc.vector.tensor_scalar(means[:], sums[0][:], 1.0 / GROUP, None, ALU.mult)
+        nc.vector.tensor_copy(
+            out=scale_dealt[:].rearrange("p s t (c i) -> p s c t i", i=16),
+            in_=scale_raw[:].rearrange("p s (c i t) -> p s c t i", i=16, t=PACK),
+        )
+        nc.vector.tensor_tensor(
+            u0_bf[:].rearrange("p (b i) t -> p b t i", i=GROUP),
+            scaled[:].rearrange("p t (b i) -> p b t i", i=GROUP),
+            means[:].rearrange("p t b -> p b t").unsqueeze(3).to_broadcast([P, J // GROUP, PACK, GROUP]),
+            ALU.subtract,
+        )
+        reach_plane(0)
+        quantise(u0_codes[:], u0_scales[:], u0_bf, E4M3)
+        for h in range(HALVES):
+            first_product(0, h)
+        pick(1, 0)
+        reach_plane(1)
+        pick(1, 1)
+        centre(slice(0, 2))
+        reach_plane(2)
+        nc.vector.tensor_copy(
+            out=scale_b_dealt[:].rearrange("p t (c i) -> p c t i", i=16),
+            in_=scale_b_raw[:].rearrange("p (c i t) -> p c t i", i=16, t=PACK),
+        )
+        for t in (2, 3):
+            pick(1, t)
+            centre(slice(t, t + 1))
+        for h in range(HALVES):
+            nc.vector.tensor_tensor(
+                woven(u1_bf[h]),
+                planar(centred[:, :, cols(h)]),
+                fk_sb[:, 1, :].unsqueeze(1).unsqueeze(3).to_broadcast([P, HALF // 4, PACK, 4]),
+                ALU.mult,
+            )
+        for h in range(HALVES):
+            quantise(u1_codes[h][:], u1_scales[h][:], u1_bf[h], E4M3)
+            first_product(1, h)
+        reach_plane(3)
+        for t in range(PACK):
+            nc.scalar.activation(floor[:, t, :], tz_win[t][:].indirect(list_floor[:]), COPY)
+
+        pre = [sbuf("pre%d" % h, [P, HALF, PACK], BF16) for h in range(HALVES)]
+        hid = [sbuf("hid%d" % h, [P, HALF, PACK], BF16) for h in range(HALVES)]
+        hid_codes = [sbuf("hid_codes%d" % h, [P, HALF], I32) for h in range(HALVES)]
+        hid_scales = [sbuf("hid_scales%d" % h, [P, HALF], U8) for h in range(HALVES)]
+        p_bank = [psum.tile([P, PACK, HALF], F32, name="p_bank%d" % h) for h in range(HALVES)]
+        for h in range(HALVES):
+            nc.vector.tensor_tensor(woven(pre[h]), planar(a_bank[h][:]), planar(reach[:, :, cols(h)]), ALU.add)
+        for h in range(HALVES):
+            nc.vector.tensor_scalar(hid[h][:], pre[h][:], 0.0, None, ALU.max)
+        for h in range(HALVES):
+            quantise(hid_codes[h][:], hid_scales[h][:], hid[h], E5M2)
+            for t in range(PACK):
+                nc.tensor.matmul_mx(
+                    out=p_bank[h][:, t, :],
+                    lhsT=wb_dealt[:, t, :].bitcast(E2M1),
+                    lhsT_scale=scale_b_dealt[:, t, :],
+                    rhs=hid_codes[h][:].bitcast(E5M2),
+                    rhs_scale=hid_scales[h][:],
+                    start=True,
+                    stop=True,
+                )
+
+        top = [sbuf("top%d" % h, [P, PACK, HALF], F32) for h in range(HALVES)]
+        y = [sbuf("y%d" % h, [P, PACK, HALF], F32) for h in range(HALVES)]
+        y_bf = [sbuf("y_bf%d" % h, [P, HALF, PACK], BF16) for h in range(HALVES)]
+        y_codes = sbuf("y_codes", [P, J], I32)
+        y_scales = sbuf("y_scales", [P, J], U8)
+        y_rows = out_0.rearrange("(p t) j -> p t j", t=PACK)
+        for h in range(HALVES):
+            nc.vector.tensor_tensor(top[h][:], p_bank[h][:], floor[:, :, cols(h)], ALU.max)
+            nc.vector.tensor_tensor(
+                y[h][:], top[h][:], rw_all[:, cols(h)].unsqueeze(1).to_broadcast([P, PACK, HALF]), ALU.mult
+            )
+            nc.sync.dma_start(out=y_rows[:, :, cols(h)], in_=y[h][:])
+        nc.scalar.copy(out=woven(y_bf[0]), in_=planar(y[0][:]))
+        nc.vector.tensor_copy(out=woven(y_bf[1]), in_=planar(y[1][:]))
+        for h in range(HALVES):
+            quantise(y_codes[:, cols(h)], y_scales[:, cols(h)], y_bf[h], E4M3)
+        nc.sync.dma_start(out=out_1[0].rearrange("p c t -> p (c t)").bitcast(I32), in_=y_codes[:])
+        for q in range(4):
+            queue = nc.scalar if q % 2 else nc.sync
+            queue.dma_start(
+                out=out_2[0, 4 * q : 4 * q + 4, :].bitcast(I32), in_=y_scales[32 * q : 32 * q + 4, :].bitcast(I32)
+            )

@@ -35,7 +35,7 @@ def tile_list_centredpicks_tworeach_floored_pl_kernel(
         psum = ctx.enter_context(tc.psum_pool(name="psum", bufs=1))
 
         def sbuf(name, shape, dtype):
-            return pool.tile(shape, dtype, name=name, align_bytes=64)
+            return pool.tile(shape, dtype, name=name, tag=name, align_bytes=64)
 
         def cols(h):
             return slice(h * HALF, (h + 1) * HALF)
@@ -46,19 +46,22 @@ def tile_list_centredpicks_tworeach_floored_pl_kernel(
         list_floor = sbuf("list_floor", [P, J // 16], U16)
 
         x_rows = xf.rearrange("(g p t) c -> g t p c", g=PASSES, t=PACK)
-        tb_rows = tb.rearrange("(p t) c -> t p c", t=PACK)
-        tz_rows = tz.rearrange("(p t) c -> t p c", t=PACK)
+        tb_pairs = tb.rearrange("(p u e) c -> u p e c", u=2, e=2)
+        tz_pairs = tz.rearrange("(p u e) c -> u p e c", u=2, e=2)
         x_win = [[sbuf("x_win%d%d" % (g, t), [P, T], F32) for t in range(PACK)] for g in range(PASSES)]
-        tb_win = [sbuf("tb_win%d" % t, [P, V], F32) for t in range(PACK)]
-        tz_win = [sbuf("tz_win%d" % t, [P, Z], F32) for t in range(PACK)]
+        tb_early = [sbuf("tb_early%d" % e, [P, V], F32) for e in range(2)]
+        tb_late = sbuf("tb_late", [P, 2, V], F32)
+        tb_win = [tb_early[0][:], tb_early[1][:], tb_late[:, 0, :], tb_late[:, 1, :]]
+        tz_pair = [sbuf("tz_pair%d" % u, [P, 2, Z], F32) for u in range(2)]
+        tz_win = [tz_pair[t // 2][:, t % 2, :] for t in range(PACK)]
         w_raw = sbuf("w_raw", [P, PASSES, R], I32)
         wb_raw = sbuf("wb_raw", [P, 2 * N], U8)
-        scale_raw = sbuf("scale_raw", [P, PASSES, R], U8)
+        scale_raw = sbuf("scale_raw", [P, R], U8)
         scale_b_raw = sbuf("scale_b_raw", [P, N], U8)
         fk_sb = sbuf("fk_sb", [P, PASSES, PACK], F32)
         rw_col = sbuf("rw_col", [P, HALVES], F32)
 
-        nc.vector.memset(scale_raw[:].rearrange("p s c -> p (s c)").bitcast(I32), 0)
+        nc.vector.memset(scale_raw[:].bitcast(I32), 0)
         nc.vector.memset(scale_b_raw[:].bitcast(I32), 0)
 
         def load_x(g, t):
@@ -66,63 +69,47 @@ def tile_list_centredpicks_tworeach_floored_pl_kernel(
 
         def load_w_scales(q):
             nc.sync.dma_start(
-                out=scale_raw[32 * q : 32 * q + 4].bitcast(I32),
-                in_=w_scales[:, 4 * q : 4 * q + 4, :].rearrange("g r c -> r g c").bitcast(I32),
+                out=scale_raw[32 * q : 32 * q + 4 * PASSES, :].bitcast(I32),
+                in_=w_scales[:, 4 * q : 4 * q + 4, :].bitcast(I32),
             )
 
         def load_wb_scales(q):
-            nc.sync.dma_start(
+            nc.gpsimd.dma_start(
                 out=scale_b_raw[32 * q : 32 * q + 4, :].bitcast(I32),
                 in_=wb_scales[0, 4 * q : 4 * q + 4, :].bitcast(I32),
             )
 
-        nc.sync.dma_start(list_x[:], offs)
-        load_x(0, 0)
-        nc.sync.dma_start(out=fk_sb[:], in_=fk.rearrange("(g p t) o -> p g (t o)", g=PASSES, t=PACK))
-        nc.sync.dma_start(out=w_raw[:], in_=w_words.rearrange("g p c t -> p g (c t)").bitcast(I32))
-        load_x(0, 1)
         nc.sync.dma_start(out=wb_raw[:].bitcast(I32), in_=wb_words[0].bitcast(I32))
-        load_w_scales(0)
-        load_x(0, 2)
-        load_w_scales(1)
-        load_w_scales(2)
-        load_x(0, 3)
-        load_w_scales(3)
         nc.sync.dma_start(list_minus[:], offs3)
-        nc.sync.dma_start(out=tb_win[0][:], in_=tb_rows[0])
+        nc.sync.dma_start(out=tb_early[0][:], in_=tb_pairs[0, :, 0, :])
         nc.sync.dma_start(list_plus[:], offs2)
+        nc.sync.dma_start(out=tb_early[1][:], in_=tb_pairs[0, :, 1, :])
+        nc.sync.dma_start(list_x[:], offs)
+        for t in range(PACK):
+            load_x(0, t)
+            load_w_scales(t)
+            load_wb_scales(t)
         load_x(1, 0)
-        load_wb_scales(0)
-        nc.sync.dma_start(out=tb_win[1][:], in_=tb_rows[1])
-        load_wb_scales(1)
-        load_x(1, 1)
-        load_wb_scales(2)
-        nc.sync.dma_start(out=tb_win[2][:], in_=tb_rows[2])
-        load_wb_scales(3)
-        load_x(1, 2)
-        load_x(1, 3)
-        nc.sync.dma_start(out=tb_win[3][:], in_=tb_rows[3])
+        nc.sync.dma_start(out=fk_sb[:], in_=fk.rearrange("(g p t) o -> p g (t o)", g=PASSES, t=PACK))
+        for t in range(1, PACK):
+            load_x(1, t)
+        nc.sync.dma_start(out=tb_late[:], in_=tb_pairs[1])
+        nc.sync.dma_start(out=w_raw[:], in_=w_words.rearrange("g p c t -> p g (c t)").bitcast(I32))
         nc.sync.dma_start(list_floor[:], offs4)
         with nc.allow_non_contiguous_dma(reason="one weight a partition"):
             nc.sync.dma_start(out=rw_col[:], in_=rw.rearrange("o (h p) -> p (o h)", h=HALVES))
-        for t in range(PACK):
-            nc.sync.dma_start(out=tz_win[t][:], in_=tz_rows[t])
+        for u in range(2):
+            nc.sync.dma_start(out=tz_pair[u][:], in_=tz_pairs[u])
 
         ident = sbuf("ident", [P, P], F32)
         make_identity(nc, ident[:])
+        warm = sbuf("warm", [P, 1], F32)
+        nc.scalar.activation(warm[:], ident[:, 0:1], COPY)
         rw_all = psum.tile([P, J], F32, name="rw_all")
         for h in range(HALVES):
             nc.tensor.transpose(rw_all[:, cols(h)], rw_col[:, h : h + 1].to_broadcast([P, P]), ident[:])
 
-        w_dealt = sbuf("w_dealt", [P, PASSES, PACK, P], I32)
         wb_dealt = sbuf("wb_dealt", [P, PACK, 2 * P], U8)
-        scale_dealt = sbuf("scale_dealt", [P, PASSES, PACK, P], U8)
-        scale_b_dealt = sbuf("scale_b_dealt", [P, PACK, P], U8)
-        for g in range(PASSES):
-            nc.vector.tensor_copy(
-                out=w_dealt[:, g].rearrange("p t (c i) -> p c t i", i=4),
-                in_=w_raw[:, g].rearrange("p (c i t) -> p c t i", i=4, t=PACK),
-            )
         nc.vector.tensor_copy(
             out=wb_dealt[:].rearrange("p t (c i b) -> p c t i b", i=8, b=2),
             in_=wb_raw[:].rearrange("p (c i t b) -> p c t i b", i=8, t=PACK, b=2),
@@ -130,116 +117,121 @@ def tile_list_centredpicks_tworeach_floored_pl_kernel(
 
         picked = [sbuf("picked%d" % g, [P, PACK, J], F32) for g in range(PASSES)]
         sums = [sbuf("sums%d" % g, [P, PACK, J // GROUP], F32) for g in range(PASSES)]
-        scaled = sbuf("scaled", [P, PACK, J], F32)
-        means = sbuf("means", [P, PACK, J // GROUP], F32)
-        centred = sbuf("centred", [P, PACK, J], F32)
+        centred = [sbuf("centred%d" % g, [P, PACK, J], F32) for g in range(PASSES)]
+        reach_row = sbuf("reach_row", [P, PACK * J], F32)
+        reach = reach_row[:].rearrange("p (t j) -> p t j", t=PACK)
         u0_bf = sbuf("u0_bf", [P, J, PACK], BF16)
+        u1_bf = reach_row[:, 2 * J :].bitcast(BF16).rearrange("p (j t) -> p j t", t=PACK)
         u0_codes = sbuf("u0_codes", [P, J], I32)
         u0_scales = sbuf("u0_scales", [P, J], U8)
-        u1_bf = [sbuf("u1_bf%d" % h, [P, HALF, PACK], BF16) for h in range(HALVES)]
         u1_codes = [sbuf("u1_codes%d" % h, [P, HALF], I32) for h in range(HALVES)]
         u1_scales = [sbuf("u1_scales%d" % h, [P, HALF], U8) for h in range(HALVES)]
         u_codes = [[u0_codes[:, cols(h)] for h in range(HALVES)], [u1_codes[h][:] for h in range(HALVES)]]
         u_scales = [[u0_scales[:, cols(h)] for h in range(HALVES)], [u1_scales[h][:] for h in range(HALVES)]]
-        minus = sbuf("minus", [P, PACK, J], F32)
-        reach = sbuf("reach", [P, PACK, J], F32)
+        minus_early = sbuf("minus_early", [P, 2, J], F32)
+        plus_late = sbuf("plus_late", [P, 2, J], F32)
+        minus_late = sbuf("minus_late", [P, 2, J], F32)
         floor = sbuf("floor", [P, PACK, J], F32)
 
-        def pick(g, t):
-            nc.scalar.activation(picked[g][:, t, :], x_win[g][t][:].indirect(list_x[:]), COPY)
+        def pick(out, window, offsets):
+            nc.scalar.activation(out, window.indirect(offsets), COPY)
 
-        def grouped(ap):
-            return ap.rearrange("p t (b i) -> p (t b) i", i=GROUP)
+        def group_sums(out, values):
+            nc.vector.tensor_reduce(out, values.rearrange("p (b i) -> p b i", i=GROUP), AXIS_X, ALU.add)
 
-        def group_sums(g, source, planes):
-            nc.vector.tensor_reduce(
-                sums[g][:, planes, :].rearrange("p t b -> p (t b)"), grouped(source[:, planes, :]), AXIS_X, ALU.add
-            )
-
-        def centre(planes):
-            group_sums(1, picked[1], planes)
-            count = (planes.stop - planes.start) * J // GROUP
+        def take_means_off(out, values, totals):
             nc.vector.scalar_tensor_tensor(
-                out=grouped(centred[:, planes, :]),
-                in0=sums[1][:, planes, :].rearrange("p t b -> p (t b)").unsqueeze(2).to_broadcast([P, count, GROUP]),
+                out=out.rearrange("p (b i) -> p b i", i=GROUP),
+                in0=totals.unsqueeze(2).to_broadcast([P, totals.shape[1], GROUP]),
                 scalar=-1.0 / GROUP,
-                in1=grouped(picked[1][:, planes, :]),
+                in1=values.rearrange("p (b i) -> p b i", i=GROUP),
                 op0=ALU.mult,
                 op1=ALU.add,
             )
 
-        def woven(tile):
-            return tile[:].rearrange("p (c i) t -> p c t i", i=4)
+        def flat(ap):
+            return ap.rearrange("p t j -> p (t j)")
+
+        def centre(g, planes):
+            for t in range(planes.start, planes.stop):
+                pick(picked[g][:, t, :], x_win[g][t][:], list_x[:])
+            group_sums(flat(sums[g][:, planes, :]), flat(picked[g][:, planes, :]))
+            take_means_off(flat(centred[g][:, planes, :]), flat(picked[g][:, planes, :]), flat(sums[g][:, planes, :]))
+
+        def woven(ap):
+            return ap.rearrange("p (c i) t -> p c t i", i=4)
 
         def planar(ap):
             return ap.rearrange("p t (c i) -> p c t i", i=4)
 
-        def quantise(codes, scales, values, fmt):
-            nc.vector.quantize_mx(out=codes.bitcast(fmt), scales=scales, in_=values[:].rearrange("p j t -> p (j t)"))
+        def weave_u(out, g, values):
+            factors = fk_sb[:, g, :].unsqueeze(1).unsqueeze(3).to_broadcast([P, values.shape[2] // 4, PACK, 4])
+            nc.vector.tensor_tensor(woven(out), planar(values), factors, ALU.mult)
 
-        def reach_plane(t):
-            nc.scalar.activation(minus[:, t, :], tb_win[t][:].indirect(list_minus[:]), COPY)
-            nc.vector.tensor_tensor(reach[:, t, :], tb_win[t][:].indirect(list_plus[:]), minus[:, t, :], ALU.subtract)
+        def quantise(codes, scales, values, fmt):
+            nc.vector.quantize_mx(out=codes.bitcast(fmt), scales=scales, in_=values.rearrange("p j t -> p (j t)"))
+
+        def deal_scales(dealt, raw):
+            nc.vector.tensor_copy(
+                out=dealt.rearrange("p t (c i) -> p c t i", i=16),
+                in_=raw[:].rearrange("p (c i t) -> p c t i", i=16, t=PACK),
+            )
 
         a_bank = [psum.tile([P, PACK, HALF], F32, name="a_bank%d" % h) for h in range(HALVES)]
 
-        def first_product(g, h):
+        def first_product(w_dealt, g, h):
             for t in range(PACK):
                 nc.tensor.matmul_mx(
                     out=a_bank[h][:, t, :],
                     lhsT=w_dealt[:, g, t, :].bitcast(E4M3),
-                    lhsT_scale=scale_dealt[:, g, t, :],
+                    lhsT_scale=scales_dealt[4 * g :, 0, t, :],
                     rhs=u_codes[g][h].bitcast(E4M3),
                     rhs_scale=u_scales[g][h],
                     start=(g == 0 and t == 0),
                     stop=(g == PASSES - 1 and t == PACK - 1),
                 )
 
-        for t in range(PACK):
-            pick(0, t)
-            nc.scalar.activation(scaled[:, t, :], picked[0][:, t, :], COPY, scale=fk_sb[:, 0, t : t + 1])
-            if t % 2:
-                group_sums(0, scaled, slice(t - 1, t + 1))
-        nc.vector.tensor_scalar(means[:], sums[0][:], 1.0 / GROUP, None, ALU.mult)
-        nc.vector.tensor_copy(
-            out=scale_dealt[:].rearrange("p s t (c i) -> p s c t i", i=16),
-            in_=scale_raw[:].rearrange("p s (c i t) -> p s c t i", i=16, t=PACK),
-        )
-        nc.vector.tensor_tensor(
-            u0_bf[:].rearrange("p (b i) t -> p b t i", i=GROUP),
-            scaled[:].rearrange("p t (b i) -> p b t i", i=GROUP),
-            means[:].rearrange("p t b -> p b t").unsqueeze(3).to_broadcast([P, J // GROUP, PACK, GROUP]),
-            ALU.subtract,
-        )
-        reach_plane(0)
-        quantise(u0_codes[:], u0_scales[:], u0_bf, E4M3)
-        for h in range(HALVES):
-            first_product(0, h)
-        pick(1, 0)
-        reach_plane(1)
-        pick(1, 1)
-        centre(slice(0, 2))
-        reach_plane(2)
-        nc.vector.tensor_copy(
-            out=scale_b_dealt[:].rearrange("p t (c i) -> p c t i", i=16),
-            in_=scale_b_raw[:].rearrange("p (c i t) -> p c t i", i=16, t=PACK),
-        )
-        for t in (2, 3):
-            pick(1, t)
-            centre(slice(t, t + 1))
-        for h in range(HALVES):
+        for t in range(2):
+            pick(minus_early[:, t, :], tb_win[t], list_minus[:])
             nc.vector.tensor_tensor(
-                woven(u1_bf[h]),
-                planar(centred[:, :, cols(h)]),
-                fk_sb[:, 1, :].unsqueeze(1).unsqueeze(3).to_broadcast([P, HALF // 4, PACK, 4]),
-                ALU.mult,
+                reach[:, t, :], tb_win[t].indirect(list_plus[:]), minus_early[:, t, :], ALU.subtract
+            )
+        scales_dealt = pool.tile([P, 2, PACK, P], U8, name="scales_dealt", tag="minus_early", align_bytes=64)
+        for t in range(PACK):
+            centre(0, slice(t, t + 1))
+            if t == 2:
+                deal_scales(scales_dealt[:, 1], scale_b_raw)
+        weave_u(u0_bf[:], 0, centred[0][:])
+        deal_scales(scales_dealt[:, 0], scale_raw)
+        quantise(u0_codes[:], u0_scales[:], u0_bf[:], E4M3)
+        for t in range(PACK - 1):
+            centre(1, slice(t, t + 1))
+        last = PACK - 1
+        half_groups = [slice(h * HALF // GROUP, (h + 1) * HALF // GROUP) for h in range(HALVES)]
+        for h in range(HALVES):
+            pick(picked[1][:, last, cols(h)], x_win[1][last][:], list_x[:, h * HALF // 16 : (h + 1) * HALF // 16])
+            group_sums(sums[1][:, last, half_groups[h]], picked[1][:, last, cols(h)])
+        for h in range(HALVES):
+            take_means_off(centred[1][:, last, cols(h)], picked[1][:, last, cols(h)], sums[1][:, last, half_groups[h]])
+        for h in range(HALVES):
+            weave_u(u1_bf[:, cols(h), :], 1, centred[1][:, :, cols(h)])
+        for h in range(HALVES):
+            quantise(u1_codes[h][:], u1_scales[h][:], u1_bf[:, cols(h), :], E4M3)
+        w_dealt = pool.tile([P, PASSES, PACK, P], I32, name="w_dealt", tag="centred1", align_bytes=64)
+        for g in range(PASSES):
+            nc.vector.tensor_copy(
+                out=w_dealt[:, g].rearrange("p t (c i) -> p c t i", i=4),
+                in_=w_raw[:, g].rearrange("p (c i t) -> p c t i", i=4, t=PACK),
             )
         for h in range(HALVES):
-            quantise(u1_codes[h][:], u1_scales[h][:], u1_bf[h], E4M3)
-            first_product(1, h)
-        reach_plane(3)
+            for g in range(PASSES):
+                first_product(w_dealt, g, h)
+        for e in range(2):
+            pick(minus_late[:, e, :], tb_win[2 + e], list_minus[:])
+            pick(plus_late[:, e, :], tb_win[2 + e], list_plus[:])
+        nc.vector.tensor_tensor(reach[:, 2:, :], plus_late[:], minus_late[:], ALU.subtract)
         for t in range(PACK):
-            nc.scalar.activation(floor[:, t, :], tz_win[t][:].indirect(list_floor[:]), COPY)
+            pick(floor[:, t, :], tz_win[t], list_floor[:])
 
         pre = [sbuf("pre%d" % h, [P, HALF, PACK], BF16) for h in range(HALVES)]
         hid = [sbuf("hid%d" % h, [P, HALF, PACK], BF16) for h in range(HALVES)]
@@ -247,16 +239,16 @@ def tile_list_centredpicks_tworeach_floored_pl_kernel(
         hid_scales = [sbuf("hid_scales%d" % h, [P, HALF], U8) for h in range(HALVES)]
         p_bank = [psum.tile([P, PACK, HALF], F32, name="p_bank%d" % h) for h in range(HALVES)]
         for h in range(HALVES):
-            nc.vector.tensor_tensor(woven(pre[h]), planar(a_bank[h][:]), planar(reach[:, :, cols(h)]), ALU.add)
+            nc.vector.tensor_tensor(woven(pre[h][:]), planar(a_bank[h][:]), planar(reach[:, :, cols(h)]), ALU.add)
         for h in range(HALVES):
             nc.vector.tensor_scalar(hid[h][:], pre[h][:], 0.0, None, ALU.max)
         for h in range(HALVES):
-            quantise(hid_codes[h][:], hid_scales[h][:], hid[h], E5M2)
+            quantise(hid_codes[h][:], hid_scales[h][:], hid[h][:], E5M2)
             for t in range(PACK):
                 nc.tensor.matmul_mx(
                     out=p_bank[h][:, t, :],
                     lhsT=wb_dealt[:, t, :].bitcast(E2M1),
-                    lhsT_scale=scale_b_dealt[:, t, :],
+                    lhsT_scale=scales_dealt[:, 1, t, :],
                     rhs=hid_codes[h][:].bitcast(E5M2),
                     rhs_scale=hid_scales[h][:],
                     start=True,
@@ -275,10 +267,10 @@ def tile_list_centredpicks_tworeach_floored_pl_kernel(
                 y[h][:], top[h][:], rw_all[:, cols(h)].unsqueeze(1).to_broadcast([P, PACK, HALF]), ALU.mult
             )
             nc.sync.dma_start(out=y_rows[:, :, cols(h)], in_=y[h][:])
-        nc.scalar.copy(out=woven(y_bf[0]), in_=planar(y[0][:]))
-        nc.vector.tensor_copy(out=woven(y_bf[1]), in_=planar(y[1][:]))
+        nc.scalar.copy(out=woven(y_bf[0][:]), in_=planar(y[0][:]))
+        nc.vector.tensor_copy(out=woven(y_bf[1][:]), in_=planar(y[1][:]))
         for h in range(HALVES):
-            quantise(y_codes[:, cols(h)], y_scales[:, cols(h)], y_bf[h], E4M3)
+            quantise(y_codes[:, cols(h)], y_scales[:, cols(h)], y_bf[h][:], E4M3)
         nc.sync.dma_start(out=out_1[0].rearrange("p c t -> p (c t)").bitcast(I32), in_=y_codes[:])
         for q in range(4):
             queue = nc.scalar if q % 2 else nc.sync

@@ -22,8 +22,14 @@ AXIS_X = mybir.AxisListType.X
 P = 128
 PACK = 4
 PASSES = K // (P * PACK)
-HALF = J // 2
 HALVES = 2
+HALF = J // HALVES
+QUAD = 32
+LIVE = 4
+STRIPE = 16
+LINE = 16
+RUN = LINE // 4
+PAIR = 2
 
 
 def tile_list_centredpicks_tworeach_floored_pl_kernel(
@@ -34,49 +40,51 @@ def tile_list_centredpicks_tworeach_floored_pl_kernel(
         pool = ctx.enter_context(tc.tile_pool(name="held", bufs=1))
         psum = ctx.enter_context(tc.psum_pool(name="psum", bufs=1))
 
-        def sbuf(name, shape, dtype):
-            return pool.tile(shape, dtype, name=name, tag=name, align_bytes=64)
+        def sbuf(name, shape, dtype, bytes_of=None):
+            return pool.tile(shape, dtype, name=name, tag=bytes_of or name, align_bytes=64)
 
         def cols(h):
             return slice(h * HALF, (h + 1) * HALF)
 
-        list_x = sbuf("list_x", [P, J // 16], U16)
-        list_plus = sbuf("list_plus", [P, J // 16], U16)
-        list_minus = sbuf("list_minus", [P, J // 16], U16)
-        list_floor = sbuf("list_floor", [P, J // 16], U16)
+        list_x = sbuf("list_x", [P, J // STRIPE], U16)
+        list_plus = sbuf("list_plus", [P, J // STRIPE], U16)
+        list_minus = sbuf("list_minus", [P, J // STRIPE], U16)
+        list_floor = sbuf("list_floor", [P, J // STRIPE], U16)
 
         x_rows = xf.rearrange("(g p t) c -> g t p c", g=PASSES, t=PACK)
-        tb_pairs = tb.rearrange("(p u e) c -> u p e c", u=2, e=2)
-        tz_pairs = tz.rearrange("(p u e) c -> u p e c", u=2, e=2)
+        tb_pairs = tb.rearrange("(p u e) c -> u p e c", u=PACK // PAIR, e=PAIR)
+        tz_pairs = tz.rearrange("(p u e) c -> u p e c", u=PACK // PAIR, e=PAIR)
         x_win = [[sbuf("x_win%d%d" % (g, t), [P, T], F32) for t in range(PACK)] for g in range(PASSES)]
-        tb_early = [sbuf("tb_early%d" % e, [P, V], F32) for e in range(2)]
-        tb_late = sbuf("tb_late", [P, 2, V], F32)
-        tb_win = [tb_early[0][:], tb_early[1][:], tb_late[:, 0, :], tb_late[:, 1, :]]
-        tz_pair = [sbuf("tz_pair%d" % u, [P, 2, Z], F32) for u in range(2)]
-        tz_win = [tz_pair[t // 2][:, t % 2, :] for t in range(PACK)]
+        tb_early = [sbuf("tb_early%d" % e, [P, V], F32) for e in range(PAIR)]
+        tb_late = sbuf("tb_late", [P, PAIR, V], F32)
+        tz_pair = [sbuf("tz_pair%d" % u, [P, PAIR, Z], F32) for u in range(PACK // PAIR)]
         w_raw = sbuf("w_raw", [P, PASSES, R], I32)
         wb_raw = sbuf("wb_raw", [P, 2 * N], U8)
-        scale_raw = sbuf("scale_raw", [P, R], U8)
-        scale_b_raw = sbuf("scale_b_raw", [P, N], U8)
+        w_scale_raw = sbuf("w_scale_raw", [P, R], U8)
+        wb_scale_raw = sbuf("wb_scale_raw", [P, N], U8)
         fk_sb = sbuf("fk_sb", [P, PASSES, PACK], F32)
         rw_col = sbuf("rw_col", [P, HALVES], F32)
 
-        nc.vector.memset(scale_raw[:].bitcast(I32), 0)
-        nc.vector.memset(scale_b_raw[:].bitcast(I32), 0)
+        warm_in = sbuf("warm_in", [P, 1], F32)
+        warm_out = sbuf("warm_out", [P, 1], F32)
+        nc.vector.memset(warm_in[:], 0.0)
+        nc.scalar.activation(warm_out[:], warm_in[:], COPY)
+        nc.vector.memset(w_scale_raw[:].bitcast(I32), 0)
+        nc.vector.memset(wb_scale_raw[:].bitcast(I32), 0)
 
         def load_x(g, t):
             nc.sync.dma_start(out=x_win[g][t][:], in_=x_rows[g, t])
 
         def load_w_scales(q):
             nc.sync.dma_start(
-                out=scale_raw[32 * q : 32 * q + 4 * PASSES, :].bitcast(I32),
-                in_=w_scales[:, 4 * q : 4 * q + 4, :].bitcast(I32),
+                out=w_scale_raw[QUAD * q : QUAD * q + LIVE * PASSES, :].bitcast(I32),
+                in_=w_scales[:, LIVE * q : LIVE * (q + 1), :].bitcast(I32),
             )
 
         def load_wb_scales(q):
-            nc.gpsimd.dma_start(
-                out=scale_b_raw[32 * q : 32 * q + 4, :].bitcast(I32),
-                in_=wb_scales[0, 4 * q : 4 * q + 4, :].bitcast(I32),
+            nc.sync.dma_start(
+                out=wb_scale_raw[QUAD * q : QUAD * q + LIVE, :].bitcast(I32),
+                in_=wb_scales[0, LIVE * q : LIVE * (q + 1), :].bitcast(I32),
             )
 
         nc.sync.dma_start(out=wb_raw[:].bitcast(I32), in_=wb_words[0].bitcast(I32))
@@ -85,52 +93,59 @@ def tile_list_centredpicks_tworeach_floored_pl_kernel(
         nc.sync.dma_start(list_plus[:], offs2)
         nc.sync.dma_start(out=tb_early[1][:], in_=tb_pairs[0, :, 1, :])
         nc.sync.dma_start(list_x[:], offs)
-        for t in range(PACK):
-            load_x(0, t)
-            load_w_scales(t)
-            load_wb_scales(t)
-        load_x(1, 0)
+        load_x(0, 0)
         nc.sync.dma_start(out=fk_sb[:], in_=fk.rearrange("(g p t) o -> p g (t o)", g=PASSES, t=PACK))
-        for t in range(1, PACK):
-            load_x(1, t)
+        load_x(0, 1)
+        load_w_scales(0)
+        load_x(0, 2)
+        load_w_scales(1)
+        load_w_scales(2)
+        load_x(0, 3)
+        load_w_scales(3)
+        load_wb_scales(0)
+        load_x(1, 0)
+        load_wb_scales(1)
+        load_wb_scales(2)
+        load_x(1, 1)
+        load_wb_scales(3)
+        with nc.allow_non_contiguous_dma(reason="one weight a partition"):
+            nc.sync.dma_start(out=rw_col[:], in_=rw.rearrange("o (h p) -> p (o h)", h=HALVES))
+        load_x(1, 2)
+        load_x(1, 3)
         nc.sync.dma_start(out=tb_late[:], in_=tb_pairs[1])
         nc.sync.dma_start(out=w_raw[:], in_=w_words.rearrange("g p c t -> p g (c t)").bitcast(I32))
         nc.sync.dma_start(list_floor[:], offs4)
-        with nc.allow_non_contiguous_dma(reason="one weight a partition"):
-            nc.sync.dma_start(out=rw_col[:], in_=rw.rearrange("o (h p) -> p (o h)", h=HALVES))
-        for u in range(2):
+        for u in range(PACK // PAIR):
             nc.sync.dma_start(out=tz_pair[u][:], in_=tz_pairs[u])
 
         ident = sbuf("ident", [P, P], F32)
         make_identity(nc, ident[:])
-        warm = sbuf("warm", [P, 1], F32)
-        nc.scalar.activation(warm[:], ident[:, 0:1], COPY)
         rw_all = psum.tile([P, J], F32, name="rw_all")
         for h in range(HALVES):
             nc.tensor.transpose(rw_all[:, cols(h)], rw_col[:, h : h + 1].to_broadcast([P, P]), ident[:])
 
         wb_dealt = sbuf("wb_dealt", [P, PACK, 2 * P], U8)
         nc.vector.tensor_copy(
-            out=wb_dealt[:].rearrange("p t (c i b) -> p c t i b", i=8, b=2),
-            in_=wb_raw[:].rearrange("p (c i t b) -> p c t i b", i=8, t=PACK, b=2),
+            out=wb_dealt[:].rearrange("p t (c i b) -> p c t i b", i=LINE // 2, b=2),
+            in_=wb_raw[:].rearrange("p (c i t b) -> p c t i b", i=LINE // 2, t=PACK, b=2),
         )
 
-        picked = [sbuf("picked%d" % g, [P, PACK, J], F32) for g in range(PASSES)]
+        scaled = [sbuf("scaled%d" % g, [P, PACK, J], F32) for g in range(PASSES)]
         sums = [sbuf("sums%d" % g, [P, PACK, J // GROUP], F32) for g in range(PASSES)]
-        centred = [sbuf("centred%d" % g, [P, PACK, J], F32) for g in range(PASSES)]
+        fk_mean = sbuf("fk_mean", [P, PASSES, PACK], F32)
         reach_row = sbuf("reach_row", [P, PACK * J], F32)
         reach = reach_row[:].rearrange("p (t j) -> p t j", t=PACK)
         u0_bf = sbuf("u0_bf", [P, J, PACK], BF16)
-        u1_bf = reach_row[:, 2 * J :].bitcast(BF16).rearrange("p (j t) -> p j t", t=PACK)
+        u1_bf = reach_row[:, PAIR * J :].bitcast(BF16).rearrange("p (j t) -> p j t", t=PACK)
         u0_codes = sbuf("u0_codes", [P, J], I32)
         u0_scales = sbuf("u0_scales", [P, J], U8)
         u1_codes = [sbuf("u1_codes%d" % h, [P, HALF], I32) for h in range(HALVES)]
         u1_scales = [sbuf("u1_scales%d" % h, [P, HALF], U8) for h in range(HALVES)]
         u_codes = [[u0_codes[:, cols(h)] for h in range(HALVES)], [u1_codes[h][:] for h in range(HALVES)]]
         u_scales = [[u0_scales[:, cols(h)] for h in range(HALVES)], [u1_scales[h][:] for h in range(HALVES)]]
-        minus_early = sbuf("minus_early", [P, 2, J], F32)
-        plus_late = sbuf("plus_late", [P, 2, J], F32)
-        minus_late = sbuf("minus_late", [P, 2, J], F32)
+        minus_early = [sbuf("minus_early%d" % e, [P, J], F32) for e in range(PAIR)]
+        plus_late = sbuf("plus_late", [P, PAIR, J], F32)
+        minus_late = sbuf("minus_late", [P, PAIR, J], F32)
         floor = sbuf("floor", [P, PACK, J], F32)
 
         def pick(out, window, offsets):
@@ -139,99 +154,105 @@ def tile_list_centredpicks_tworeach_floored_pl_kernel(
         def group_sums(out, values):
             nc.vector.tensor_reduce(out, values.rearrange("p (b i) -> p b i", i=GROUP), AXIS_X, ALU.add)
 
-        def take_means_off(out, values, totals):
-            nc.vector.scalar_tensor_tensor(
-                out=out.rearrange("p (b i) -> p b i", i=GROUP),
-                in0=totals.unsqueeze(2).to_broadcast([P, totals.shape[1], GROUP]),
-                scalar=-1.0 / GROUP,
-                in1=values.rearrange("p (b i) -> p b i", i=GROUP),
-                op0=ALU.mult,
-                op1=ALU.add,
-            )
-
-        def flat(ap):
-            return ap.rearrange("p t j -> p (t j)")
-
-        def centre(g, planes):
-            for t in range(planes.start, planes.stop):
-                pick(picked[g][:, t, :], x_win[g][t][:], list_x[:])
-            group_sums(flat(sums[g][:, planes, :]), flat(picked[g][:, planes, :]))
-            take_means_off(flat(centred[g][:, planes, :]), flat(picked[g][:, planes, :]), flat(sums[g][:, planes, :]))
+        def take_plane(g, t):
+            picked = sbuf("picked%d%d" % (g, t), [P, J], F32)
+            pick(picked[:], x_win[g][t][:], list_x[:])
+            group_sums(sums[g][:, t, :], picked[:])
+            nc.gpsimd.tensor_scalar(scaled[g][:, t, :], picked[:], fk_sb[:, g, t : t + 1], 0.0, ALU.mult, ALU.add)
 
         def woven(ap):
-            return ap.rearrange("p (c i) t -> p c t i", i=4)
+            return ap.rearrange("p (c i) t -> p c t i", i=RUN)
 
         def planar(ap):
-            return ap.rearrange("p t (c i) -> p c t i", i=4)
+            return ap.rearrange("p t (c i) -> p c t i", i=RUN)
 
-        def weave_u(out, g, values):
-            factors = fk_sb[:, g, :].unsqueeze(1).unsqueeze(3).to_broadcast([P, values.shape[2] // 4, PACK, 4])
-            nc.vector.tensor_tensor(woven(out), planar(values), factors, ALU.mult)
+        def scaled_means(name, g, totals):
+            groups = totals.shape[2]
+            runs = GROUP // RUN
+            means = sbuf(name, [P, runs * groups, PACK], F32)
+            nc.vector.tensor_tensor(
+                means[:].rearrange("p (b e) t -> p b e t", e=runs),
+                totals.rearrange("p t b -> p b t").unsqueeze(2).to_broadcast([P, groups, runs, PACK]),
+                fk_mean[:, g, :].unsqueeze(1).unsqueeze(1).to_broadcast([P, groups, runs, PACK]),
+                ALU.mult,
+            )
+            return means
+
+        def centre(out, values, means):
+            spread = means[:].unsqueeze(3).to_broadcast([P, means.shape[1], PACK, RUN])
+            nc.vector.tensor_tensor(woven(out), planar(values), spread, ALU.subtract)
 
         def quantise(codes, scales, values, fmt):
             nc.vector.quantize_mx(out=codes.bitcast(fmt), scales=scales, in_=values.rearrange("p j t -> p (j t)"))
 
         def deal_scales(dealt, raw):
             nc.vector.tensor_copy(
-                out=dealt.rearrange("p t (c i) -> p c t i", i=16),
-                in_=raw[:].rearrange("p (c i t) -> p c t i", i=16, t=PACK),
+                out=dealt[:].rearrange("p t (c i) -> p c t i", i=LINE),
+                in_=raw[:].rearrange("p (c i t) -> p c t i", i=LINE, t=PACK),
             )
 
         a_bank = [psum.tile([P, PACK, HALF], F32, name="a_bank%d" % h) for h in range(HALVES)]
 
-        def first_product(w_dealt, g, h):
-            for t in range(PACK):
-                nc.tensor.matmul_mx(
-                    out=a_bank[h][:, t, :],
-                    lhsT=w_dealt[:, g, t, :].bitcast(E4M3),
-                    lhsT_scale=scales_dealt[4 * g :, 0, t, :],
-                    rhs=u_codes[g][h].bitcast(E4M3),
-                    rhs_scale=u_scales[g][h],
-                    start=(g == 0 and t == 0),
-                    stop=(g == PASSES - 1 and t == PACK - 1),
-                )
-
-        for t in range(2):
-            pick(minus_early[:, t, :], tb_win[t], list_minus[:])
+        for e in range(PAIR):
+            pick(minus_early[e][:], tb_early[e][:], list_minus[:])
             nc.vector.tensor_tensor(
-                reach[:, t, :], tb_win[t].indirect(list_plus[:]), minus_early[:, t, :], ALU.subtract
+                reach[:, e, :], tb_early[e][:].indirect(list_plus[:]), minus_early[e][:], ALU.subtract
             )
-        scales_dealt = pool.tile([P, 2, PACK, P], U8, name="scales_dealt", tag="minus_early", align_bytes=64)
+
+        w_scale_dealt = sbuf("w_scale_dealt", [P, PACK, P], U8, bytes_of="minus_early1")
+        nc.gpsimd.tensor_scalar(fk_mean[:], fk_sb[:], 1.0 / GROUP, 0.0, ALU.mult, ALU.add)
         for t in range(PACK):
-            centre(0, slice(t, t + 1))
-            if t == 2:
-                deal_scales(scales_dealt[:, 1], scale_b_raw)
-        weave_u(u0_bf[:], 0, centred[0][:])
-        deal_scales(scales_dealt[:, 0], scale_raw)
+            take_plane(0, t)
+        centre(u0_bf[:], scaled[0][:], scaled_means("means0", 0, sums[0][:]))
+        deal_scales(w_scale_dealt, w_scale_raw)
         quantise(u0_codes[:], u0_scales[:], u0_bf[:], E4M3)
-        for t in range(PACK - 1):
-            centre(1, slice(t, t + 1))
+
         last = PACK - 1
+        take_plane(1, 0)
+        take_plane(1, 1)
+        wb_scale_dealt = sbuf("wb_scale_dealt", [P, PACK, P], U8, bytes_of="u0_bf")
+        deal_scales(wb_scale_dealt, wb_scale_raw)
+        take_plane(1, 2)
         half_groups = [slice(h * HALF // GROUP, (h + 1) * HALF // GROUP) for h in range(HALVES)]
         for h in range(HALVES):
-            pick(picked[1][:, last, cols(h)], x_win[1][last][:], list_x[:, h * HALF // 16 : (h + 1) * HALF // 16])
-            group_sums(sums[1][:, last, half_groups[h]], picked[1][:, last, cols(h)])
+            picked_last = sbuf("picked_last%d" % h, [P, HALF], F32)
+            pick(picked_last[:], x_win[1][last][:], list_x[:, h * HALF // STRIPE : (h + 1) * HALF // STRIPE])
+            group_sums(sums[1][:, last, half_groups[h]], picked_last[:])
+            nc.vector.tensor_scalar(
+                scaled[1][:, last, cols(h)], picked_last[:], fk_sb[:, 1, last : last + 1], None, ALU.mult
+            )
+        means1 = [scaled_means("means1%d" % h, 1, sums[1][:, :, half_groups[h]]) for h in range(HALVES)]
         for h in range(HALVES):
-            take_means_off(centred[1][:, last, cols(h)], picked[1][:, last, cols(h)], sums[1][:, last, half_groups[h]])
-        for h in range(HALVES):
-            weave_u(u1_bf[:, cols(h), :], 1, centred[1][:, :, cols(h)])
+            centre(u1_bf[:, cols(h), :], scaled[1][:, :, cols(h)], means1[h])
         for h in range(HALVES):
             quantise(u1_codes[h][:], u1_scales[h][:], u1_bf[:, cols(h), :], E4M3)
-        w_dealt = pool.tile([P, PASSES, PACK, P], I32, name="w_dealt", tag="centred1", align_bytes=64)
+
+        w_dealt = sbuf("w_dealt", [P, PASSES, PACK, P], I32, bytes_of="scaled1")
         for g in range(PASSES):
             nc.vector.tensor_copy(
-                out=w_dealt[:, g].rearrange("p t (c i) -> p c t i", i=4),
-                in_=w_raw[:, g].rearrange("p (c i t) -> p c t i", i=4, t=PACK),
+                out=w_dealt[:, g].rearrange("p t (c i) -> p c t i", i=RUN),
+                in_=w_raw[:, g].rearrange("p (c i t) -> p c t i", i=RUN, t=PACK),
             )
+
         for h in range(HALVES):
             for g in range(PASSES):
-                first_product(w_dealt, g, h)
-        for e in range(2):
-            pick(minus_late[:, e, :], tb_win[2 + e], list_minus[:])
-            pick(plus_late[:, e, :], tb_win[2 + e], list_plus[:])
-        nc.vector.tensor_tensor(reach[:, 2:, :], plus_late[:], minus_late[:], ALU.subtract)
+                for t in range(PACK):
+                    nc.tensor.matmul_mx(
+                        out=a_bank[h][:, t, :],
+                        lhsT=w_dealt[:, g, t, :].bitcast(E4M3),
+                        lhsT_scale=w_scale_dealt[LIVE * g :, t, :],
+                        rhs=u_codes[g][h].bitcast(E4M3),
+                        rhs_scale=u_scales[g][h],
+                        start=(g == 0 and t == 0),
+                        stop=(g == PASSES - 1 and t == PACK - 1),
+                    )
+
+        for e in range(PAIR):
+            pick(minus_late[:, e, :], tb_late[:, e, :], list_minus[:])
+            pick(plus_late[:, e, :], tb_late[:, e, :], list_plus[:])
+        nc.vector.tensor_tensor(reach[:, PAIR:, :], plus_late[:], minus_late[:], ALU.subtract)
         for t in range(PACK):
-            pick(floor[:, t, :], tz_win[t], list_floor[:])
+            pick(floor[:, t, :], tz_pair[t // PAIR][:, t % PAIR, :], list_floor[:])
 
         pre = [sbuf("pre%d" % h, [P, HALF, PACK], BF16) for h in range(HALVES)]
         hid = [sbuf("hid%d" % h, [P, HALF, PACK], BF16) for h in range(HALVES)]
@@ -248,7 +269,7 @@ def tile_list_centredpicks_tworeach_floored_pl_kernel(
                 nc.tensor.matmul_mx(
                     out=p_bank[h][:, t, :],
                     lhsT=wb_dealt[:, t, :].bitcast(E2M1),
-                    lhsT_scale=scales_dealt[:, 1, t, :],
+                    lhsT_scale=wb_scale_dealt[:, t, :],
                     rhs=hid_codes[h][:].bitcast(E5M2),
                     rhs_scale=hid_scales[h][:],
                     start=True,
@@ -272,8 +293,9 @@ def tile_list_centredpicks_tworeach_floored_pl_kernel(
         for h in range(HALVES):
             quantise(y_codes[:, cols(h)], y_scales[:, cols(h)], y_bf[h][:], E4M3)
         nc.sync.dma_start(out=out_1[0].rearrange("p c t -> p (c t)").bitcast(I32), in_=y_codes[:])
-        for q in range(4):
+        for q in range(P // QUAD):
             queue = nc.scalar if q % 2 else nc.sync
             queue.dma_start(
-                out=out_2[0, 4 * q : 4 * q + 4, :].bitcast(I32), in_=y_scales[32 * q : 32 * q + 4, :].bitcast(I32)
+                out=out_2[0, LIVE * q : LIVE * (q + 1), :].bitcast(I32),
+                in_=y_scales[QUAD * q : QUAD * q + LIVE, :].bitcast(I32),
             )

from contextlib import ExitStack

import concourse.mybir as mybir
from concourse.masks import make_identity

K, T, J, R, V, N, Z = 1024, 1024, 256, 512, 512, 512, 512
GROUP = 8
FLOPS = 2 * K * R * J + 2 * R * N * J

F32 = mybir.dt.float32
BF16 = mybir.dt.bfloat16
I32 = mybir.dt.int32
U16 = mybir.dt.uint16
U8 = mybir.dt.uint8
E4M3 = mybir.dt.float8_e4m3fn_x4
E5M2 = mybir.dt.float8_e5m2_x4
E2M1 = mybir.dt.float4_e2m1fn_x4
ALU = mybir.AluOpType
COPY = mybir.ActivationFunctionType.Copy
AXIS_X = mybir.AxisListType.X

P = 128
PACK = 4
PASSES = K // (P * PACK)
HALVES = 2
HALF = J // HALVES
QUAD = 32
LIVE = 4
STRIPE = 16
LINE = 16
RUN = LINE // 4
PAIR = 2


def tile_list_centredpicks_tworeach_floored_pl_kernel(
    tc, xf, fk, w_words, w_scales, tb, wb_words, wb_scales, tz, rw, offs, offs2, offs3, offs4, out_0, out_1, out_2
):
    nc = tc.nc
    with ExitStack() as ctx:
        pool = ctx.enter_context(tc.tile_pool(name="held", bufs=1))
        psum = ctx.enter_context(tc.psum_pool(name="psum", bufs=1))

        def sbuf(name, shape, dtype, bytes_of=None):
            return pool.tile(shape, dtype, name=name, tag=bytes_of or name, align_bytes=64)

        def cols(h):
            return slice(h * HALF, (h + 1) * HALF)

        list_x = sbuf("list_x", [P, J // STRIPE], U16)
        list_plus = sbuf("list_plus", [P, J // STRIPE], U16)
        list_minus = sbuf("list_minus", [P, J // STRIPE], U16)
        list_floor = sbuf("list_floor", [P, J // STRIPE], U16)

        x_rows = xf.rearrange("(g p t) c -> g t p c", g=PASSES, t=PACK)
        tb_pairs = tb.rearrange("(p u e) c -> u p e c", u=PACK // PAIR, e=PAIR)
        tz_pairs = tz.rearrange("(p u e) c -> u p e c", u=PACK // PAIR, e=PAIR)
        x_win = [[sbuf("x_win%d%d" % (g, t), [P, T], F32) for t in range(PACK)] for g in range(PASSES)]
        tb_early = [sbuf("tb_early%d" % e, [P, V], F32) for e in range(PAIR)]
        tb_late = sbuf("tb_late", [P, PAIR, V], F32)
        tz_pair = [sbuf("tz_pair%d" % u, [P, PAIR, Z], F32) for u in range(PACK // PAIR)]
        w_raw = sbuf("w_raw", [P, PASSES, R], I32)
        wb_raw = sbuf("wb_raw", [P, 2 * N], U8)
        w_scale_raw = sbuf("w_scale_raw", [P, R], U8)
        wb_scale_raw = sbuf("wb_scale_raw", [P, N], U8)
        fk_sb = sbuf("fk_sb", [P, PASSES, PACK], F32)
        rw_col = sbuf("rw_col", [P, HALVES], F32)

        warm_in = sbuf("warm_in", [P, 1], F32)
        warm_out = sbuf("warm_out", [P, 1], F32)
        nc.vector.memset(warm_in[:], 0.0)
        nc.scalar.activation(warm_out[:], warm_in[:], COPY)
        nc.vector.memset(w_scale_raw[:].bitcast(I32), 0)
        nc.vector.memset(wb_scale_raw[:].bitcast(I32), 0)

        def load_x(g, t):
            nc.sync.dma_start(out=x_win[g][t][:], in_=x_rows[g, t])

        def load_w_scales(q):
            nc.sync.dma_start(
                out=w_scale_raw[QUAD * q : QUAD * q + LIVE * PASSES, :].bitcast(I32),
                in_=w_scales[:, LIVE * q : LIVE * (q + 1), :].bitcast(I32),
            )

        def load_wb_scales(q):
            nc.sync.dma_start(
                out=wb_scale_raw[QUAD * q : QUAD * q + LIVE, :].bitcast(I32),
                in_=wb_scales[0, LIVE * q : LIVE * (q + 1), :].bitcast(I32),
            )

        nc.sync.dma_start(out=wb_raw[:].bitcast(I32), in_=wb_words[0].bitcast(I32))
        nc.sync.dma_start(list_minus[:], offs3)
        nc.sync.dma_start(out=tb_early[0][:], in_=tb_pairs[0, :, 0, :])
        nc.sync.dma_start(list_plus[:], offs2)
        nc.sync.dma_start(out=tb_early[1][:], in_=tb_pairs[0, :, 1, :])
        nc.sync.dma_start(list_x[:], offs)
        load_x(0, 0)
        nc.sync.dma_start(out=fk_sb[:], in_=fk.rearrange("(g p t) o -> p g (t o)", g=PASSES, t=PACK))
        load_x(0, 1)
        load_w_scales(0)
        load_x(0, 2)
        load_w_scales(1)
        load_w_scales(2)
        load_x(0, 3)
        load_w_scales(3)
        load_wb_scales(0)
        load_x(1, 0)
        load_wb_scales(1)
        load_wb_scales(2)
        load_x(1, 1)
        load_wb_scales(3)
        with nc.allow_non_contiguous_dma(reason="one weight a partition"):
            nc.sync.dma_start(out=rw_col[:], in_=rw.rearrange("o (h p) -> p (o h)", h=HALVES))
        load_x(1, 2)
        load_x(1, 3)
        nc.sync.dma_start(out=tb_late[:], in_=tb_pairs[1])
        nc.sync.dma_start(out=w_raw[:], in_=w_words.rearrange("g p c t -> p g (c t)").bitcast(I32))
        nc.sync.dma_start(list_floor[:], offs4)
        for u in range(PACK // PAIR):
            nc.sync.dma_start(out=tz_pair[u][:], in_=tz_pairs[u])

        ident = sbuf("ident", [P, P], F32)
        make_identity(nc, ident[:])
        rw_all = psum.tile([P, J], F32, name="rw_all")
        for h in range(HALVES):
            nc.tensor.transpose(rw_all[:, cols(h)], rw_col[:, h : h + 1].to_broadcast([P, P]), ident[:])

        wb_dealt = sbuf("wb_dealt", [P, PACK, 2 * P], U8)
        nc.vector.tensor_copy(
            out=wb_dealt[:].rearrange("p t (c i b) -> p c t i b", i=LINE // 2, b=2),
            in_=wb_raw[:].rearrange("p (c i t b) -> p c t i b", i=LINE // 2, t=PACK, b=2),
        )

        scaled = [sbuf("scaled%d" % g, [P, PACK, J], F32) for g in range(PASSES)]
        sums = [sbuf("sums%d" % g, [P, PACK, J // GROUP], F32) for g in range(PASSES)]
        fk_mean = sbuf("fk_mean", [P, PASSES, PACK], F32)
        reach_row = sbuf("reach_row", [P, PACK * J], F32)
        reach = reach_row[:].rearrange("p (t j) -> p t j", t=PACK)
        u0_bf = sbuf("u0_bf", [P, J, PACK], BF16)
        u1_bf = reach_row[:, PAIR * J :].bitcast(BF16).rearrange("p (j t) -> p j t", t=PACK)
        u0_codes = sbuf("u0_codes", [P, J], I32)
        u0_scales = sbuf("u0_scales", [P, J], U8)
        u1_codes = [sbuf("u1_codes%d" % h, [P, HALF], I32) for h in range(HALVES)]
        u1_scales = [sbuf("u1_scales%d" % h, [P, HALF], U8) for h in range(HALVES)]
        u_codes = [[u0_codes[:, cols(h)] for h in range(HALVES)], [u1_codes[h][:] for h in range(HALVES)]]
        u_scales = [[u0_scales[:, cols(h)] for h in range(HALVES)], [u1_scales[h][:] for h in range(HALVES)]]
        minus_early = [sbuf("minus_early%d" % e, [P, J], F32) for e in range(PAIR)]
        plus_late = sbuf("plus_late", [P, PAIR, J], F32)
        minus_late = sbuf("minus_late", [P, PAIR, J], F32)
        floor = sbuf("floor", [P, PACK, J], F32)

        def pick(out, window, offsets):
            nc.scalar.activation(out, window.indirect(offsets), COPY)

        def group_sums(out, values):
            nc.vector.tensor_reduce(out, values.rearrange("p (b i) -> p b i", i=GROUP), AXIS_X, ALU.add)

        def take_plane(g, t):
            picked = sbuf("picked%d%d" % (g, t), [P, J], F32)
            pick(picked[:], x_win[g][t][:], list_x[:])
            group_sums(sums[g][:, t, :], picked[:])
            nc.gpsimd.tensor_scalar(scaled[g][:, t, :], picked[:], fk_sb[:, g, t : t + 1], 0.0, ALU.mult, ALU.add)

        def woven(ap):
            return ap.rearrange("p (c i) t -> p c t i", i=RUN)

        def planar(ap):
            return ap.rearrange("p t (c i) -> p c t i", i=RUN)

        def scaled_means(name, g, totals):
            groups = totals.shape[2]
            runs = GROUP // RUN
            means = sbuf(name, [P, runs * groups, PACK], F32)
            nc.vector.tensor_tensor(
                means[:].rearrange("p (b e) t -> p b e t", e=runs),
                totals.rearrange("p t b -> p b t").unsqueeze(2).to_broadcast([P, groups, runs, PACK]),
                fk_mean[:, g, :].unsqueeze(1).unsqueeze(1).to_broadcast([P, groups, runs, PACK]),
                ALU.mult,
            )
            return means

        def centre(out, values, means):
            spread = means[:].unsqueeze(3).to_broadcast([P, means.shape[1], PACK, RUN])
            nc.vector.tensor_tensor(woven(out), planar(values), spread, ALU.subtract)

        def quantise(codes, scales, values, fmt):
            nc.vector.quantize_mx(out=codes.bitcast(fmt), scales=scales, in_=values.rearrange("p j t -> p (j t)"))

        def deal_scales(dealt, raw):
            nc.vector.tensor_copy(
                out=dealt[:].rearrange("p t (c i) -> p c t i", i=LINE),
                in_=raw[:].rearrange("p (c i t) -> p c t i", i=LINE, t=PACK),
            )

        a_bank = [psum.tile([P, PACK, HALF], F32, name="a_bank%d" % h) for h in range(HALVES)]

        for e in range(PAIR):
            pick(minus_early[e][:], tb_early[e][:], list_minus[:])
            nc.vector.tensor_tensor(
                reach[:, e, :], tb_early[e][:].indirect(list_plus[:]), minus_early[e][:], ALU.subtract
            )

        w_scale_dealt = sbuf("w_scale_dealt", [P, PACK, P], U8, bytes_of="minus_early1")
        nc.gpsimd.tensor_scalar(fk_mean[:], fk_sb[:], 1.0 / GROUP, 0.0, ALU.mult, ALU.add)
        for t in range(PACK):
            take_plane(0, t)
        centre(u0_bf[:], scaled[0][:], scaled_means("means0", 0, sums[0][:]))
        deal_scales(w_scale_dealt, w_scale_raw)
        quantise(u0_codes[:], u0_scales[:], u0_bf[:], E4M3)

        last = PACK - 1
        take_plane(1, 0)
        take_plane(1, 1)
        wb_scale_dealt = sbuf("wb_scale_dealt", [P, PACK, P], U8, bytes_of="u0_bf")
        deal_scales(wb_scale_dealt, wb_scale_raw)
        take_plane(1, 2)
        half_groups = [slice(h * HALF // GROUP, (h + 1) * HALF // GROUP) for h in range(HALVES)]
        for h in range(HALVES):
            picked_last = sbuf("picked_last%d" % h, [P, HALF], F32)
            pick(picked_last[:], x_win[1][last][:], list_x[:, h * HALF // STRIPE : (h + 1) * HALF // STRIPE])
            group_sums(sums[1][:, last, half_groups[h]], picked_last[:])
            nc.vector.tensor_scalar(
                scaled[1][:, last, cols(h)], picked_last[:], fk_sb[:, 1, last : last + 1], None, ALU.mult
            )
        means1 = [scaled_means("means1%d" % h, 1, sums[1][:, :, half_groups[h]]) for h in range(HALVES)]
        for h in range(HALVES):
            centre(u1_bf[:, cols(h), :], scaled[1][:, :, cols(h)], means1[h])
        for h in range(HALVES):
            quantise(u1_codes[h][:], u1_scales[h][:], u1_bf[:, cols(h), :], E4M3)

        w_dealt = sbuf("w_dealt", [P, PASSES, PACK, P], I32, bytes_of="scaled1")
        for g in range(PASSES):
            nc.vector.tensor_copy(
                out=w_dealt[:, g].rearrange("p t (c i) -> p c t i", i=RUN),
                in_=w_raw[:, g].rearrange("p (c i t) -> p c t i", i=RUN, t=PACK),
            )

        for h in range(HALVES):
            for g in range(PASSES):
                for t in range(PACK):
                    nc.tensor.matmul_mx(
                        out=a_bank[h][:, t, :],
                        lhsT=w_dealt[:, g, t, :].bitcast(E4M3),
                        lhsT_scale=w_scale_dealt[LIVE * g :, t, :],
                        rhs=u_codes[g][h].bitcast(E4M3),
                        rhs_scale=u_scales[g][h],
                        start=(g == 0 and t == 0),
                        stop=(g == PASSES - 1 and t == PACK - 1),
                    )

        for e in range(PAIR):
            pick(minus_late[:, e, :], tb_late[:, e, :], list_minus[:])
            pick(plus_late[:, e, :], tb_late[:, e, :], list_plus[:])
        nc.vector.tensor_tensor(reach[:, PAIR:, :], plus_late[:], minus_late[:], ALU.subtract)
        for t in range(PACK):
            pick(floor[:, t, :], tz_pair[t // PAIR][:, t % PAIR, :], list_floor[:])

        pre = [sbuf("pre%d" % h, [P, HALF, PACK], BF16) for h in range(HALVES)]
        hid = [sbuf("hid%d" % h, [P, HALF, PACK], BF16) for h in range(HALVES)]
        hid_codes = [sbuf("hid_codes%d" % h, [P, HALF], I32) for h in range(HALVES)]
        hid_scales = [sbuf("hid_scales%d" % h, [P, HALF], U8) for h in range(HALVES)]
        p_bank = [psum.tile([P, PACK, HALF], F32, name="p_bank%d" % h) for h in range(HALVES)]
        for h in range(HALVES):
            nc.vector.tensor_tensor(woven(pre[h][:]), planar(a_bank[h][:]), planar(reach[:, :, cols(h)]), ALU.add)
        for h in range(HALVES):
            nc.vector.tensor_scalar(hid[h][:], pre[h][:], 0.0, None, ALU.max)
        for h in range(HALVES):
            quantise(hid_codes[h][:], hid_scales[h][:], hid[h][:], E5M2)
            for t in range(PACK):
                nc.tensor.matmul_mx(
                    out=p_bank[h][:, t, :],
                    lhsT=wb_dealt[:, t, :].bitcast(E2M1),
                    lhsT_scale=wb_scale_dealt[:, t, :],
                    rhs=hid_codes[h][:].bitcast(E5M2),
                    rhs_scale=hid_scales[h][:],
                    start=True,
                    stop=True,
                )

        top = [sbuf("top%d" % h, [P, PACK, HALF], F32) for h in range(HALVES)]
        y = [sbuf("y%d" % h, [P, PACK, HALF], F32) for h in range(HALVES)]
        y_bf = [sbuf("y_bf%d" % h, [P, HALF, PACK], BF16) for h in range(HALVES)]
        y_codes = sbuf("y_codes", [P, J], I32)
        y_scales = sbuf("y_scales", [P, J], U8)
        y_rows = out_0.rearrange("(p t) j -> p t j", t=PACK)
        for h in range(HALVES):
            nc.vector.tensor_tensor(top[h][:], p_bank[h][:], floor[:, :, cols(h)], ALU.max)
            nc.vector.tensor_tensor(
                y[h][:], top[h][:], rw_all[:, cols(h)].unsqueeze(1).to_broadcast([P, PACK, HALF]), ALU.mult
            )
            nc.sync.dma_start(out=y_rows[:, :, cols(h)], in_=y[h][:])
        nc.scalar.copy(out=woven(y_bf[0][:]), in_=planar(y[0][:]))
        nc.vector.tensor_copy(out=woven(y_bf[1][:]), in_=planar(y[1][:]))
        for h in range(HALVES):
            quantise(y_codes[:, cols(h)], y_scales[:, cols(h)], y_bf[h][:], E4M3)
        nc.sync.dma_start(out=out_1[0].rearrange("p c t -> p (c t)").bitcast(I32), in_=y_codes[:])
        for q in range(P // QUAD):
            queue = nc.scalar if q % 2 else nc.sync
            queue.dma_start(
                out=out_2[0, LIVE * q : LIVE * (q + 1), :].bitcast(I32),
                in_=y_scales[QUAD * q : QUAD * q + LIVE, :].bitcast(I32),
            )
